import numpy as np
import ml_dtypes


def mxq(x, axis, fmt="e4m3"):
    dtype, down = {"e4m3": (ml_dtypes.float8_e4m3fn, 7), "e5m2": (ml_dtypes.float8_e5m2, 14)}[fmt]
    v = np.moveaxis(np.asarray(x, np.float32).astype(ml_dtypes.bfloat16).astype(np.float64), axis, -1)
    blocks = v.reshape(v.shape[:-1] + (-1, 32))
    amax = np.abs(blocks).max(-1, keepdims=True)
    byte = np.maximum(np.where(amax > 0, np.frexp(amax)[1] - 1 + 127, 0) - down, 1)
    scale = np.exp2(byte - 127.0)
    codes = (blocks / scale).astype(np.float32).astype(dtype).astype(np.float64)
    return np.moveaxis((codes * scale).reshape(v.shape), -1, axis)


WIDE = False


def mx_kscale(k):
    if not WIDE:
        return np.ones(k)
    levels = np.array([10, -10, 5, -5, 0])
    if k % 512:
        return np.exp2(np.random.permutation(np.resize(levels, k // 32))).repeat(32)
    a = np.empty((k // 512, 16))
    for p in range(k // 512):
        a[p, :8] = np.random.permutation(np.resize(levels, 8))
        for g in range(8):
            far = levels[np.abs(levels - a[p, g]) >= 10]
            a[p, g + 8] = far[np.random.randint(len(far))]
    return np.exp2(a.ravel()).repeat(32)


def f64(x):
    return np.asarray(x).astype(np.float64)


def striped(idx):
    return np.tile(idx.reshape(-1, 16).T, (8, 1)).astype(np.uint16)


def unstriped(offs):
    return offs[:16].T.reshape(-1).astype(np.int64)


def pack_weight(w):
    k, n = w.shape
    w = f64(np.asarray(w, np.float32).astype(ml_dtypes.bfloat16)).reshape(k // 32, 32, n)
    amax = np.abs(w).max(1)
    byte = np.clip(np.where(amax > 0, np.frexp(amax)[1] - 1 + 127 - 7, 1), 1, 254)
    scaled = (w * np.exp2(127.0 - byte)[:, None, :]).reshape(k, n).astype(np.float32)
    words = np.ascontiguousarray(scaled.reshape(k // 512, 128, 4, n).transpose(0, 1, 3, 2)).astype(ml_dtypes.float8_e4m3fn).view(np.uint8)
    return words, np.ascontiguousarray(byte.astype(np.uint8).reshape(k // 512, 16, n))


def unpack_weight(words, scales):
    g, p, n, _ = words.shape
    vals = np.ascontiguousarray(words).view(ml_dtypes.float8_e4m3fn).astype(np.float64) * np.repeat(np.exp2(scales.astype(np.float64) - 127.0), 8, axis=1)[..., None]
    return vals.transpose(0, 1, 3, 2).reshape(g * 512, n)


K, T, S, N, U, V = 512, 2048, 512, 128, 512, 256
P = 2 ** 7


def setup_inputs():
    n = np.random.standard_normal
    s = mx_kscale(K)[:, None]
    packed_xT = pack_weight(n((K, T)) * s)
    return {
        "x_words": packed_xT[0],
        "x_scales": packed_xT[1],
        "w1": (n((K, N)) / np.sqrt(K) / s).astype(np.float32),
        "pipe": (np.tile(np.random.uniform(0.5, 1.5, U), (P, 1))).astype(np.float32),
        "dem": (np.random.uniform(0.0, 1.5, (N, V))).astype(np.float32),
        "offs": striped(np.random.permutation(T)[:S]),
        "fr": striped(np.random.randint(0, S, U)),
        "to": striped(np.random.randint(0, S, U)),
        "ina": striped(np.random.permutation(U)[:V]),
        "inb": striped(np.random.permutation(U)[:V]),
        "outa": striped(np.random.permutation(U)[:V]),
    }


def reference(x_words, x_scales, w1, pipe, dem, offs, fr, to, ina, inb, outa):
    xq = unpack_weight(x_words, x_scales)[:, unstriped(offs)]
    y = mxq(f64(w1), 0, "e4m3").T @ xq
    pres = np.log(np.exp(y) + 1.0) + 0.3
    dp = (pres[:, unstriped(fr)]) ** 2 - ((pres[:, unstriped(to)]) ** 2)
    flow = (f64(pipe)[:1] * dp) / (np.sqrt(np.abs(dp) + 0.1))
    return flow[:, unstriped(ina)] + flow[:, unstriped(inb)] - flow[:, unstriped(outa)] - f64(dem)

from contextlib import ExitStack

import concourse.mybir as mybir

F32 = mybir.dt.float32
BF16 = mybir.dt.bfloat16
I32 = mybir.dt.int32
U32 = mybir.dt.uint32
U16 = mybir.dt.uint16
U8 = mybir.dt.uint8
FP8X4 = mybir.dt.float8_e4m3fn_x4
ACT = mybir.ActivationFunctionType
ALU = mybir.AluOpType

P = 128
PACK = 4
T = 2048
S = 512
U = 512
V = 256
M = 128
HALF = 256
FLOPS = 2 * 512 * M * S
EXP_CAP = 2.0 ** 40


def entries(lst, a, b):
    return lst[:, a // 16 : b // 16]


def tile_picked_yweymth_bal_p_kernel(tc, x_words, x_scales, w1, pipe, dem, offs, fr, to, ina, inb, outa, out):
    nc = tc.nc
    with ExitStack() as ctx:
        sb = ctx.enter_context(tc.tile_pool(name="sb", bufs=1))
        ps = ctx.enter_context(tc.psum_pool(name="ps", bufs=1))

        offs_sb = sb.tile([P, S // 16], U16, name="offs_sb")
        fr_sb = sb.tile([P, U // 16], U16, name="fr_sb")
        to_sb = sb.tile([P, U // 16], U16, name="to_sb")
        ina_sb = sb.tile([P, V // 16], U16, name="ina_sb")
        inb_sb = sb.tile([P, V // 16], U16, name="inb_sb")
        outa_sb = sb.tile([P, V // 16], U16, name="outa_sb")

        scale_table = sb.tile([P, T], U8, name="scale_table", align_bytes=64)
        nc.vector.memset(scale_table[:].bitcast(I32), 0)

        w_raw = sb.tile([P, PACK, M], F32, name="w_raw")
        word_table = sb.tile([P, T], I32, name="word_table", align_bytes=64)
        pipe_sb = sb.tile([P, U], F32, name="pipe_sb")
        dem_sb = sb.tile([P, V], F32, name="dem_sb")
        nc.sync.dma_start(offs_sb[:], offs)
        nc.sync.dma_start(out=w_raw[:], in_=w1.rearrange("(p j) m -> p j m", j=PACK))
        words_hbm = x_words[0].rearrange("p c r -> p (c r)").bitcast(I32)
        nc.sync.dma_start(out=word_table[:, : T // 2], in_=words_hbm[:, : T // 2])
        for q in range(4):
            nc.sync.dma_start(
                out=scale_table[32 * q : 32 * q + 4, :].bitcast(I32),
                in_=x_scales[0, 4 * q : 4 * q + 4, :].bitcast(I32),
            )
        nc.sync.dma_start(to_sb[:], to)
        nc.sync.dma_start(out=word_table[:, T // 2 :], in_=words_hbm[:, T // 2 :])
        nc.sync.dma_start(fr_sb[:], fr)
        nc.sync.dma_start(out=pipe_sb[:], in_=pipe)
        nc.sync.dma_start(outa_sb[:], outa)
        nc.sync.dma_start(ina_sb[:], ina)
        nc.sync.dma_start(inb_sb[:], inb)
        nc.sync.dma_start(out=dem_sb[:], in_=dem)

        w_grouped = sb.tile([P, M, PACK], BF16, name="w_grouped", align_bytes=64)
        nc.scalar.activation(w_grouped[:], w_raw[:].rearrange("p j m -> p m j"), ACT.Copy)
        w_codes = sb.tile([P, M], U32, name="w_codes", align_bytes=64)
        w_scales = sb.tile([P, M], U8, name="w_scales", align_bytes=64)

        x_bytes = sb.tile([P, S], U8, name="x_bytes", align_bytes=64)
        nc.vector.tensor_copy(x_bytes[:], scale_table[:].indirect(offs_sb[:]))
        nc.vector.quantize_mx(
            out=w_codes[:].bitcast(FP8X4),
            scales=w_scales[:],
            in_=w_grouped[:].rearrange("p m j -> p (m j)"),
        )

        halves = [slice(h * HALF, (h + 1) * HALF) for h in range(2)]
        x_codes = [sb.tile([P, HALF], U32, name="x_codes%d" % h, align_bytes=64) for h in range(2)]
        y = [ps.tile([P, HALF], F32, name="y%d" % h) for h in range(2)]
        grow = sb.tile([P, S], F32, name="grow")
        capped = sb.tile([P, S], F32, name="capped")
        linear = sb.tile([P, S], F32, name="linear")
        soft = sb.tile([P, S], F32, name="soft")
        pres = sb.tile([P, S], F32, name="pres")
        pres_sq = sb.tile([P, S], F32, name="pres_sq")

        for h, c in enumerate(halves):
            nc.vector.tensor_copy(
                x_codes[h][:], word_table[:].bitcast(U32).indirect(entries(offs_sb, c.start, c.stop))
            )
        for h, c in enumerate(halves):
            nc.tensor.matmul_mx(
                out=y[h][:],
                lhsT=w_codes[:].bitcast(FP8X4),
                lhsT_scale=w_scales[:],
                rhs=x_codes[h][:].bitcast(FP8X4),
                rhs_scale=x_bytes[:, c],
                start=True,
                stop=True,
            )
        for h, c in enumerate(halves):
            nc.scalar.activation(grow[:, c], y[h][:], ACT.Exp)
        for h, c in enumerate(halves):
            nc.vector.tensor_scalar(capped[:, c], grow[:, c], EXP_CAP, None, op0=ALU.min)
        for h, c in enumerate(halves):
            nc.vector.tensor_scalar(linear[:, c], y[h][:], 0.3, None, op0=ALU.add)
        for h, c in enumerate(halves):
            nc.scalar.activation(soft[:, c], capped[:, c], ACT.Ln, bias=1.0)
        for h, c in enumerate(halves):
            nc.vector.scalar_tensor_tensor(pres[:, c], soft[:, c], 0.3, linear[:, c], op0=ALU.add, op1=ALU.max)
        nc.vector.tensor_tensor(pres_sq[:, halves[0]], pres[:, halves[0]], pres[:, halves[0]], ALU.mult)
        nc.scalar.activation(pres_sq[:, halves[1]], pres[:, halves[1]], ACT.Square)

        warm = sb.tile([P, 1], F32, name="warm")
        nc.scalar.activation(warm[:], pres_sq[:, S - 1 : S], ACT.Abs_reciprocal_sqrt)
        sq_to = sb.tile([P, U], F32, name="sq_to")
        dp = sb.tile([P, U], F32, name="dp")
        size = sb.tile([P, U], F32, name="size")
        inv_root = sb.tile([P, U], F32, name="inv_root")
        scaled = sb.tile([P, U], F32, name="scaled")
        flow = sb.tile([P, U], F32, name="flow")
        for c in halves:
            nc.vector.tensor_copy(sq_to[:, c], pres_sq[:].indirect(entries(to_sb, c.start, c.stop)))
        for c in halves:
            nc.vector.tensor_tensor(
                dp[:, c], pres_sq[:].indirect(entries(fr_sb, c.start, c.stop)), sq_to[:, c], ALU.subtract
            )
        for c in halves:
            nc.scalar.activation(size[:, c], dp[:, c], ACT.Abs)
            nc.scalar.activation(inv_root[:, c], size[:, c], ACT.Abs_reciprocal_sqrt, bias=0.1)
        for c in halves:
            nc.vector.tensor_tensor(scaled[:, c], dp[:, c], pipe_sb[:, c], ALU.mult)
        for c in halves:
            nc.vector.tensor_tensor(flow[:, c], scaled[:, c], inv_root[:, c], ALU.mult)

        leaving = sb.tile([P, V], F32, name="leaving")
        part = sb.tile([P, V], F32, name="part")
        res = sb.tile([P, V], F32, name="res")
        nodes = [slice(0, V // 2), slice(V // 2, V)]
        for c in nodes:
            nc.vector.tensor_tensor(
                leaving[:, c], flow[:].indirect(entries(outa_sb, c.start, c.stop)), dem_sb[:, c], ALU.add
            )
        for c in nodes:
            nc.vector.tensor_tensor(
                part[:, c], flow[:].indirect(entries(ina_sb, c.start, c.stop)), leaving[:, c], ALU.subtract
            )
        for c in nodes:
            nc.vector.tensor_tensor(
                res[:, c], flow[:].indirect(entries(inb_sb, c.start, c.stop)), part[:, c], ALU.add
            )
            nc.sync.dma_start(out=out[:, c], in_=res[:, c])
